import numpy as np, ml_dtypes
CORES = [33,38,57,62,81,86,161,166,185,190,209,214]
N = 12
TK = 512
def setup_inputs(rng):
    return {"b": rng.standard_normal((N, 128, TK), dtype=np.float32).astype(ml_dtypes.bfloat16), "l": (rng.standard_normal((N, 128, N * 128), dtype=np.float32) / 16).astype(ml_dtypes.bfloat16)}
def setup_inputs_big(rng):
    d = setup_inputs(rng)
    for k in ("b",): d[k] = (d[k].astype(np.float32) * 1048576.0).astype(d[k].dtype)
    return d
def setup_inputs_small(rng):
    d = setup_inputs(rng)
    for k in ("b",): d[k] = (d[k].astype(np.float32) * (1 / 1048576.0)).astype(d[k].dtype)
    return d
def setup_inputs_apart(rng):
    d = setup_inputs(rng)
    f = (10.0 ** rng.permutation(np.linspace(-1.5, 1.5, N))).astype(np.float32).reshape(N, 1, 1)
    for k in ("b",): d[k] = (d[k].astype(np.float32) * f).astype(d[k].dtype)
    return d
def reference(b, l):
    B, L = b.astype(np.float64), l.astype(np.float64)
    y = np.zeros((N, 128, TK))
    for r in range(N):
        acc = B[r].copy()
        for s in range(r):
            acc -= L[s][:, 128 * r:128 * r + 128].T @ y[s]
        y[r] = acc
    return {"y": y.astype(ml_dtypes.bfloat16)}

@@ -1,0 +1,417 @@
+import comms_topo
+from concourse.bass import DstId, RemoteDMATransfer
+from concourse.mybir import AluOpType
+
+N = 12
+TK = 512
+TS = 128
+NCORES = 256
+CORES = [33, 38, 57, 62, 81, 86, 161, 166, 185, 190, 209, 214]
+
+GROUPS = [[0, 1], [2, 3, 4, 5], [6, 7, 8, 9], [10, 11]]
+HOME = [1, 5, 9, 11]
+P = 4
+PG = [4, 4, 4, 4]
+C = 4
+EXTRA = {}
+RELAY = "helper"
+TFWD = True
+FUSE = True
+CAP_ON, CAP_OFF = 16, 8
+RET_FINE = True
+NOM = (0.7, 1.8, 2.0e5, 1.0e5, 1.5)
+
+
+def _bits(m):
+    return [i for i in range(32) if (m >> i) & 1]
+
+
+def _build():
+    topo = comms_topo
+    W, CD, DW = TK // C, C // P, TK // P
+    ops, tok, semn, tlp, bbp = [], {}, {}, {}, {}
+
+    def col(r, c):
+        return ((c // CD) * N + r) * DW + (c % CD) * W
+
+    def newsem(cores):
+        i = max(semn.get(c, 0) for c in cores)
+        for c in cores:
+            semn[c] = i + 1
+        return i
+
+    def addop(**kw):
+        kw["id"] = len(ops)
+        kw.setdefault("deps", [])
+        ops.append(kw)
+        return kw
+
+    def chipof(a):
+        return (topo.host(a), topo.chip(a))
+
+    def samechip(a, b):
+        return chipof(a) == chipof(b)
+
+    def relay_of(src, dst):
+        cand = [c for c in range(NCORES) if c != src and samechip(c, src) and topo.may_write(c, dst)]
+        if RELAY == "rank":
+            pref = [c for c in cand if c in CORES]
+        else:
+            pref = [c for c in cand if c not in CORES and topo.die(c) == topo.die(src)]
+        return (pref or cand)[0]
+
+    def width(spec):
+        return (spec[3] - spec[2] + 1) * TS if spec[0] == "tl" else spec[-1] - spec[-2]
+
+    def present(core, spec):
+        if spec[0] == "bb":
+            bbp.setdefault(core, set()).add(spec[1])
+        elif spec[0] == "tl":
+            for r in range(spec[2], spec[3] + 1):
+                tlp.setdefault(core, set()).add((spec[1], r))
+
+    def sendm(items, src):
+        if not FUSE and len(items) > 1:
+            for it in items:
+                sendm([it], src)
+            return
+        byspec, m = {}, -1
+        for keys, spec, dst in items:
+            byspec.setdefault(spec, (keys, []))[1].append(dst)
+            m &= topo.mask(src, dst)
+        on = all(samechip(src, it[2]) for it in items)
+        cap, ne = min(len(_bits(m)), CAP_ON if on else CAP_OFF), 1
+        while ne * 2 * len(byspec) <= cap:
+            ne *= 2
+        op = addop(core=src, q="g", kind="send", deps=sorted({(src, k) for it in items for k in it[0]}), trs=[], on=on,
+                   dst=items[0][2], bytes=sum(width(it[1]) * 256 for it in items))
+        for i, (spec, (keys, dsts)) in enumerate(byspec.items()):
+            sem = newsem(dsts)
+            op["trs"].append({"spec": spec, "dsts": dsts, "sem": sem, "ne": ne, "off": i * ne})
+            for d in dsts:
+                for k in keys:
+                    assert (d, k) not in tok, (d, k)
+                    tok[(d, k)] = (sem, ne, [op["id"]])
+                present(d, spec)
+
+    def bychip(items, src):
+        grp = {}
+        for it in items:
+            grp.setdefault(chipof(it[2]), []).append(it)
+        for its in grp.values():
+            sendm(its, src)
+
+    def fan(items, src):
+        items = [it for it in items if not all((it[2], k) in tok for k in it[0])]
+        bychip([it for it in items if topo.may_write(src, it[2])], src)
+        rel = {}
+        for it in items:
+            if not topo.may_write(src, it[2]):
+                rel.setdefault(relay_of(src, it[2]), []).append(it)
+        for rl, its in rel.items():
+            fan(list({it[1]: (it[0], it[1], rl) for it in its}.values()), src)
+            bychip(its, rl)
+
+    def xfer(keys, spec, src, dst):
+        fan([(keys, spec, dst)], src)
+
+    def load(core, q, keys, spec, src):
+        sem = newsem([core])
+        op = addop(core=core, q=q, kind="load", spec=spec, src=src, sem=sem, bytes=width(spec) * 256)
+        for k in keys:
+            tok[(core, k)] = (sem, 16, [op["id"]])
+        present(core, spec)
+
+    def runs(rows):
+        out = []
+        for r in sorted(rows):
+            if out and out[-1][1] == r - 1:
+                out[-1][1] = r
+            else:
+                out.append([r, r])
+        return out
+
+    rows_at, doms_at, sol, gidx = {}, {}, [], {}
+    for gi, rows in enumerate(GROUPS):
+        lead = CORES[HOME[gi]]
+        free = [c for c in range(NCORES) if samechip(c, lead) and c not in CORES
+                and all(topo.may_write(c, d) for d in CORES)]
+        od = [c for c in free if topo.die(c) != topo.die(lead)]
+        sd = [c for c in free if topo.die(c) == topo.die(lead)]
+        seq = [lead] + [x for pair in zip(od, sd + od) for x in pair]
+        sol.append([seq[j * PG[gi] // P] for j in range(P)])
+        for j, x in enumerate(sol[gi]):
+            rows_at[x] = list(rows)
+            doms_at.setdefault(x, []).append(j)
+        for r in rows:
+            gidx[r] = gi
+    solvers = list(rows_at)
+    for rank, rows in EXTRA.items():
+        rows_at[CORES[rank]] = list(rows)
+        doms_at[CORES[rank]] = list(range(P))
+
+    def chunks(j):
+        return range(j * CD, (j + 1) * CD)
+
+    for r in range(N):
+        o = CORES[r]
+        if r == 0:
+            for j in range(P):
+                load(o, ("sync", "scalar")[j % 2], [("Y", 0, c) for c in chunks(j)], ("yy", col(0, j * CD), col(0, j * CD) + DW),
+                     ("b", j * DW, (j + 1) * DW))
+        else:
+            load(o, "sync", [("B", r, j) for j in range(P)], ("bb", r, 0, TK), ("b", 0, TK))
+        if r < N - 1:
+            cut = GROUPS[min(gidx[r] + 1, len(GROUPS) - 1)][-1]
+            for q, a, b in (("scalar", r + 1, cut), ("sync", cut + 1, N - 1)):
+                if a <= b:
+                    load(o, q, [("T", r, x) for x in range(a, b + 1)], ("tl", r, a, b), ("l", a * TS, (b + 1) * TS))
+
+    for s in range(N - 1):
+        src = CORES[s]
+        first, later = {}, []
+
+        def route(d, need):
+            if topo.may_write(src, d):
+                first.setdefault(d, set()).update(need)
+            else:
+                rl = relay_of(src, d)
+                first.setdefault(rl, set()).update(need)
+                later.append((rl, d, need))
+
+        sets = [sorted(set(x)) for x in sol] + [[CORES[k]] for k in EXTRA]
+        for dset in sets:
+            need = [r for r in rows_at[dset[0]] if r > s]
+            dset = [d for d in dset if d != src]
+            if not need or not dset:
+                continue
+            if TFWD and len(dset) > 1 and not samechip(src, dset[0]):
+                ld = dset[s % len(dset)]
+                route(ld, need)
+                later.extend((ld, d, need) for d in dset if d != ld)
+            else:
+                for d in dset:
+                    route(d, need)
+        calls = {}
+        for f, d, rows in [(src, d, rows) for d, rows in first.items()] + later:
+            for a, b in runs(rows):
+                calls.setdefault((f, a, b, chipof(d)), []).append(([("T", s, x) for x in range(a, b + 1)], ("tl", s, a, b), d))
+        for k, its in calls.items():
+            sendm(its, k[0])
+
+    for k in range(CD):
+        fan([([("Y", 0, j * CD + k)], ("yy", col(0, j * CD + k), col(0, j * CD + k) + W), d)
+             for d, rows in rows_at.items() if 0 in rows and d != CORES[0] for j in doms_at[d]], CORES[0])
+    for r in range(1, N):
+        fan([([("B", r, j)], ("bb", r, j * DW, (j + 1) * DW), d)
+             for d, rows in rows_at.items() if r in rows and d != CORES[r] for j in doms_at[d]], CORES[r])
+
+    for x, rows in rows_at.items():
+        comp = [r for r in rows if r > 0]
+        cs = [c for j in doms_at[x] for c in chunks(j)]
+        nb = 8 // len(cs)
+        for i, r in enumerate(comp):
+            for ci, c in enumerate(cs):
+                sem, ids, bank = newsem([x]), [], (i % nb) * len(cs) + ci
+                for s in range(r):
+                    deps = [(x, ("T", s, r)), (x, ("Y", s, c))]
+                    if i >= nb:
+                        deps.append((x, ("Y", comp[i - nb], c)))
+                    ids.append(addop(core=x, q="tensor", kind="mm", r=r, s=s, c=c, bank=bank, sem=sem, deps=deps)["id"])
+                tok[(x, ("A", r, c))] = (sem, r, ids)
+                ysem = newsem([x])
+                op = addop(core=x, q="vector", kind="sub", r=r, c=c, bank=bank, sem=ysem,
+                           deps=[(x, ("A", r, c)), (x, ("B", r, c // CD))])
+                tok[(x, ("Y", r, c))] = (ysem, 1, [op["id"]])
+
+    for gi, rows in enumerate(GROUPS):
+        for j in range(P):
+            p = sol[gi][j]
+            for d, drows in rows_at.items():
+                if d == p or j not in doms_at[d]:
+                    continue
+                need = [s for s in rows if s not in drows and s < max(drows) and not (s == 0 and d == CORES[0])]
+                if not need:
+                    continue
+                if min(drows) - 1 in rows:
+                    for c in chunks(j):
+                        for s in need:
+                            xfer([("Y", s, c)], ("yy", col(s, c), col(s, c) + W), p, d)
+                else:
+                    via = [q for q in solvers if d not in solvers and q != p and samechip(q, d) and j in doms_at[q]
+                           and max(need) < min(rows_at[q])]
+                    for a, b in runs(need):
+                        xfer([("Y", s, c) for s in range(a, b + 1) for c in chunks(j)],
+                             ("yy", col(a, j * CD), col(b, j * CD) + DW), (via or [p])[0], d)
+            for s in rows:
+                o = CORES[s]
+                if s == 0 or (o, ("Y", s, j * CD)) in tok:
+                    continue
+                if RET_FINE:
+                    for c in chunks(j):
+                        xfer([("Y", s, c)], ("yy", col(s, c), col(s, c) + W), p, o)
+                else:
+                    xfer([("Y", s, c) for c in chunks(j)], ("yy", col(s, j * CD), col(s, j * CD) + DW), p, o)
+
+    for r in range(N):
+        o, c, k = CORES[r], 0, 0
+        while c < C:
+            e = c
+            while e + 1 < C and (e + 1) // CD == c // CD and tok[(o, ("Y", r, e + 1))][0] == tok[(o, ("Y", r, c))][0]:
+                e += 1
+            addop(core=o, q=("sync", "scalar")[k % 2], kind="store", a=c * W, b=(e + 1) * W, ya=col(r, c),
+                  deps=[(o, ("Y", r, c))], bytes=(e + 1 - c) * W * 256)
+            c, k = e + 1, k + 1
+
+    n = len(ops)
+    par = [sorted({i for d in op["deps"] for i in tok[d][2]}) for op in ops]
+    chi = [[] for _ in ops]
+    for i, ps in enumerate(par):
+        for p in ps:
+            chi[p].append(i)
+
+    def busy(op):
+        k = op["kind"]
+        return NOM[0] if k == "send" else W / 1400.0 + 0.06 if k == "mm" else W / 960.0 + 0.06 if k == "sub" else 0.05
+
+    def tail(op):
+        k = op["kind"]
+        if k == "send":
+            return NOM[1] + op["bytes"] / (NOM[2] if op["on"] else NOM[3])
+        return 2.0 + op["bytes"] / 3.0e5 if k in ("load", "store") else 0.1
+
+    indeg = [len(p) for p in par]
+    topo_order = [i for i in range(n) if indeg[i] == 0]
+    for i in topo_order:
+        for ch in chi[i]:
+            indeg[ch] -= 1
+            if indeg[ch] == 0:
+                topo_order.append(ch)
+    assert len(topo_order) == n
+    bl = [0.0] * n
+    for i in reversed(topo_order):
+        bl[i] = busy(ops[i]) + tail(ops[i]) + max([bl[ch] for ch in chi[i]] or [0.0])
+    indeg = [len(p) for p in par]
+    ready = {i: 0.0 for i in range(n) if indeg[i] == 0}
+    rdy, qfree, engfree, prog, span = [0.0] * n, {}, {}, {}, [0.0]
+    while ready:
+        best = min(ready, key=lambda i: (max(ready[i], qfree.get((ops[i]["core"], ops[i]["q"]), 0.0)), -bl[i], i))
+        op = ops[best]
+        qk = (op["core"], op["q"])
+        st = max(ready.pop(best), qfree.get(qk, 0.0))
+        if op["kind"] == "send":
+            if qk not in qfree:
+                st += NOM[4]
+            port = op["core"] if op["on"] else chipof(op["dst"]) + (topo.die(op["core"]),)
+            beg = max(st + busy(op), engfree.get(op["core"], 0.0), engfree.get(port, 0.0))
+            engfree[op["core"]] = engfree[port] = beg + tail(op) - NOM[1]
+            done = beg + tail(op)
+        else:
+            done = st + busy(op) + tail(op)
+        qfree[qk] = st + busy(op)
+        span[0] = max(span[0], done)
+        op["t0"], op["t1"] = st, done
+        prog.setdefault(op["core"], {}).setdefault(op["q"], []).append(op)
+        for ch in chi[best]:
+            rdy[ch] = max(rdy[ch], done)
+            indeg[ch] -= 1
+            if indeg[ch] == 0:
+                ready[ch] = rdy[ch]
+
+    for core, qs in prog.items():
+        seen, last = set(), {}
+        for op in qs.get("tensor", []):
+            k = (op["r"], op["c"])
+            op["start"] = k not in seen
+            op["stop"] = False
+            seen.add(k)
+            last[k] = op
+        for op in last.values():
+            op["stop"] = True
+    for op in ops:
+        op["waits"] = sorted({tok[d][:2] for d in op["deps"]})
+        if op["kind"] in ("mm", "sub"):
+            op["yc"] = col(op["s"] if op["kind"] == "mm" else op["r"], op["c"])
+    tls = {c: {k: i for i, k in enumerate(sorted(v))} for c, v in tlp.items()}
+    bbs = {c: {k: i for i, k in enumerate(sorted(v))} for c, v in bbp.items()}
+    return {"span": span[0], "prog": prog, "tls": tls, "bbs": bbs, "nsem": max(semn.values()), "W": W,
+            "tln": max(len(v) for v in tls.values()), "bbn": max(len(v) for v in bbs.values()),
+            "banks": 1 + max(op["bank"] for op in ops if op["kind"] == "mm")}
+
+
+_P = _build()
+
+SCRATCH = {
+    "yy": ("sbuf", [128, N * TK], "bfloat16"),
+    "bb": ("sbuf", [128, _P["bbn"] * TK], "bfloat16"),
+    "tl": ("sbuf", [128, _P["tln"] * TS], "bfloat16"),
+}
+for _i in range(_P["banks"]):
+    SCRATCH["ps%d" % _i] = ("psum", [128, 512], "float32")
+SEMAPHORES = ["sent", "stsync", "stscalar"] + ["s%d" % _i for _i in range(_P["nsem"])]
+
+
+def rank_program(g, core, T, topo):
+    prog = _P["prog"].get(core)
+    if not prog:
+        return
+    W = _P["W"]
+    queues = {"g": g, "tensor": g.tensor, "vector": g.vector, "sync": g.sync, "scalar": g.scalar}
+
+    def ap(c, spec):
+        if spec[0] == "yy":
+            return T.yy[:, spec[1]:spec[2]]
+        if spec[0] == "bb":
+            k = _P["bbs"][c][spec[1]] * TK
+            return T.bb[:, k + spec[2]:k + spec[3]]
+        k = _P["tls"][c][(spec[1], spec[2])]
+        return T.tl[:, k * TS:(k + spec[3] - spec[2] + 1) * TS]
+
+    for qn, lst in prog.items():
+        q, waited, sent, stored = queues[qn], {}, 0, 0
+        for op in lst:
+            for sem, val in op["waits"]:
+                if waited.get(sem, 0) < val:
+                    q.wait_ge(T.sem["s%d" % sem], val)
+                    waited[sem] = val
+            kind = op["kind"]
+            if kind == "load":
+                src = T.b if op["src"][0] == "b" else T.l
+                q.dma_start(ap(core, op["spec"]), src[:, op["src"][1]:op["src"][2]]).then_inc(T.sem["s%d" % op["sem"]], 16)
+            elif kind == "store":
+                q.dma_start(T.y[:, op["a"]:op["b"]], T.yy[:, op["ya"]:op["ya"] + op["b"] - op["a"]]).then_inc(T.sem["st" + qn], 16)
+                stored += 16
+            elif kind == "send":
+                m = -1
+                for tr in op["trs"]:
+                    for d in tr["dsts"]:
+                        m &= topo.mask(core, d)
+                eng, trs = _bits(m), []
+                for tr in op["trs"]:
+                    mask = sum(1 << e for e in eng[tr["off"]:tr["off"] + tr["ne"]])
+                    sent += tr["ne"]
+                    if len(op["trs"]) == 1 and len(tr["dsts"]) == 1:
+                        rid, pid = topo.addr(tr["dsts"][0], core)
+                        q.remote_dma(out_ap=ap(tr["dsts"][0], tr["spec"]), in_ap=ap(core, tr["spec"]),
+                                     remote_sem=T.sem["s%d" % tr["sem"]], local_sem=T.sem.sent, pid=pid, routing_id=rid,
+                                     dma_engine_mask=mask)
+                    else:
+                        ids = [topo.addr(d, core) for d in tr["dsts"]]
+                        trs.append(RemoteDMATransfer(dst_ids=[DstId(rid=a, pnc=b) for a, b in ids], dma_engine_mask=mask,
+                                                     remote_sem=T.sem["s%d" % tr["sem"]], srcs=[ap(core, tr["spec"])],
+                                                     dsts=[ap(d, tr["spec"]) for d in tr["dsts"]], alu_op=0))
+                if trs:
+                    q.remote_dma_fused(trs, local_sem=T.sem.sent)
+            elif kind == "mm":
+                k = _P["tls"][core][(op["s"], op["r"])]
+                q.matmul(T["ps%d" % op["bank"]][:, 0:W], T.tl[:, k * TS:(k + 1) * TS], T.yy[:, op["yc"]:op["yc"] + W],
+                         start=op["start"], stop=op["stop"]).then_inc(T.sem["s%d" % op["sem"]], 1)
+            else:
+                k = _P["bbs"][core][op["r"]] * TK + op["c"] * W
+                q.tensor_tensor(out=T.yy[:, op["yc"]:op["yc"] + W], in0=T.bb[:, k:k + W],
+                                in1=T["ps%d" % op["bank"]][:, 0:W], op=AluOpType.subtract
+                                ).then_inc(T.sem["s%d" % op["sem"]], 1)
+        if sent:
+            q.wait_ge(T.sem.sent, sent)
+        if stored:
+            q.wait_ge(T.sem["st" + qn], stored)

@@ -8,10 +8,10 @@ TS = 128
 NCORES = 256
 CORES = [33, 38, 57, 62, 81, 86, 161, 166, 185, 190, 209, 214]
 
-GROUPS = [[0, 1], [2, 3, 4, 5], [6, 7, 8, 9], [10, 11]]
-HOME = [1, 5, 9, 11]
+GROUPS = [[0, 1, 2, 3, 4, 5, 6], [7, 8, 9, 10, 11]]
+HOME = [1, -1]
 P = 4
-PG = [4, 4, 4, 4]
+PG = [4, 4]
 C = 4
 EXTRA = {}
 RELAY = "helper"
@@ -19,7 +19,13 @@ TFWD = True
 FUSE = True
 CAP_ON, CAP_OFF = 16, 8
 RET_FINE = True
-NOM = (0.7, 1.8, 2.0e5, 1.0e5, 1.5)
+SEGS = [[1, 2], [3, 4], [5, 6], [7, 8], [9, 11]]
+DIRECT = []
+YRUNS = None
+PAIR = True
+DIEFWD = True
+RELAY2 = False
+NOM = (0.4, 1.2, 4.0e5, 2.0e5, 1.0, 1.5)
 
 
 def _bits(m):
@@ -52,13 +58,24 @@ def _build():
     def samechip(a, b):
         return chipof(a) == chipof(b)
 
-    def relay_of(src, dst):
+    def relay_of(src, dst, alt=False):
         cand = [c for c in range(NCORES) if c != src and samechip(c, src) and topo.may_write(c, dst)]
         if RELAY == "rank":
             pref = [c for c in cand if c in CORES]
         else:
             pref = [c for c in cand if c not in CORES and topo.die(c) == topo.die(src)]
-        return (pref or cand)[0]
+        return (pref or cand)[-1 if alt and RELAY2 else 0]
+
+    def links(src, dst):
+        if samechip(src, dst):
+            return []
+        d = topo.die(src)
+        if topo.same_plane(src, dst):
+            return [("out", chipof(src), d), ("in", chipof(dst), d)]
+        mt = chipof([c for c in range(NCORES) if topo.mates(c, src)][0])
+        if mt == chipof(dst):
+            return [("mate", chipof(src), d)]
+        return [("mate", chipof(src), d), ("out", mt, d), ("in", chipof(dst), d)]
 
     def width(spec):
         return (spec[3] - spec[2] + 1) * TS if spec[0] == "tl" else spec[-1] - spec[-2]
@@ -84,7 +101,10 @@ def _build():
         while ne * 2 * len(byspec) <= cap:
             ne *= 2
         op = addop(core=src, q="g", kind="send", deps=sorted({(src, k) for it in items for k in it[0]}), trs=[], on=on,
-                   dst=items[0][2], bytes=sum(width(it[1]) * 256 for it in items))
+                   dst=items[0][2], bytes=sum(width(it[1]) * 256 for it in items), lk={})
+        for it in items:
+            for l in links(src, it[2]):
+                op["lk"][l] = op["lk"].get(l, 0) + width(it[1]) * 256
         for i, (spec, (keys, dsts)) in enumerate(byspec.items()):
             sem = newsem(dsts)
             op["trs"].append({"spec": spec, "dsts": dsts, "sem": sem, "ne": ne, "off": i * ne})
@@ -133,12 +153,18 @@ def _build():
 
     rows_at, doms_at, sol, gidx = {}, {}, [], {}
     for gi, rows in enumerate(GROUPS):
-        lead = CORES[HOME[gi]]
+        lead = CORES[abs(HOME[gi])]
+        if HOME[gi] < 0:
+            lead = [c for c in range(NCORES) if topo.mates(c, lead)][0]
         free = [c for c in range(NCORES) if samechip(c, lead) and c not in CORES
                 and all(topo.may_write(c, d) for d in CORES)]
         od = [c for c in free if topo.die(c) != topo.die(lead)]
         sd = [c for c in free if topo.die(c) == topo.die(lead)]
         seq = [lead] + [x for pair in zip(od, sd + od) for x in pair]
+        if HOME[gi] < 0:
+            seq = []
+            for j in range(P):
+                seq.append([c for c in free if c not in seq and topo.die(c) == topo.die(sol[0][j])][0])
         sol.append([seq[j * PG[gi] // P] for j in range(P)])
         for j, x in enumerate(sol[gi]):
             rows_at[x] = list(rows)
@@ -162,8 +188,8 @@ def _build():
         else:
             load(o, "sync", [("B", r, j) for j in range(P)], ("bb", r, 0, TK), ("b", 0, TK))
         if r < N - 1:
-            cut = GROUPS[min(gidx[r] + 1, len(GROUPS) - 1)][-1]
-            for q, a, b in (("scalar", r + 1, cut), ("sync", cut + 1, N - 1)):
+            for i, (a, b) in enumerate([(max(x[0], r + 1), x[1]) for x in SEGS if x[1] > r]):
+                q = ("scalar", "sync")[i % 2]
                 if a <= b:
                     load(o, q, [("T", r, x) for x in range(a, b + 1)], ("tl", r, a, b), ("l", a * TS, (b + 1) * TS))
 
@@ -173,27 +199,30 @@ def _build():
 
         def route(d, need):
             if topo.may_write(src, d):
-                first.setdefault(d, set()).update(need)
+                first.setdefault((d, need[0]), set()).update(need)
             else:
-                rl = relay_of(src, d)
-                first.setdefault(rl, set()).update(need)
+                rl = relay_of(src, d, True)
+                first.setdefault((rl, need[0]), set()).update(need)
                 later.append((rl, d, need))
 
         sets = [sorted(set(x)) for x in sol] + [[CORES[k]] for k in EXTRA]
-        for dset in sets:
-            need = [r for r in rows_at[dset[0]] if r > s]
+        for dset, seg in [(x, y) for x in sets for y in SEGS]:
+            need = [r for r in rows_at[dset[0]] if r > s and seg[0] <= r <= seg[1]]
             dset = [d for d in dset if d != src]
             if not need or not dset:
                 continue
-            if TFWD and len(dset) > 1 and not samechip(src, dset[0]):
+            if TFWD and len(dset) > 1 and not samechip(src, dset[0]) and (s, seg[0]) not in DIRECT:
                 ld = dset[s % len(dset)]
+                if DIEFWD:
+                    cd = [d for d in dset if topo.die(d) == topo.die(src)]
+                    ld = cd[(s // 2 + seg[0]) % len(cd)]
                 route(ld, need)
                 later.extend((ld, d, need) for d in dset if d != ld)
             else:
                 for d in dset:
                     route(d, need)
         calls = {}
-        for f, d, rows in [(src, d, rows) for d, rows in first.items()] + later:
+        for f, d, rows in [(src, d[0], rows) for d, rows in first.items()] + later:
             for a, b in runs(rows):
                 calls.setdefault((f, a, b, chipof(d)), []).append(([("T", s, x) for x in range(a, b + 1)], ("tl", s, a, b), d))
         for k, its in calls.items():
@@ -235,14 +264,21 @@ def _build():
                     continue
                 if min(drows) - 1 in rows:
                     for c in chunks(j):
-                        for s in need:
-                            xfer([("Y", s, c)], ("yy", col(s, c), col(s, c) + W), p, d)
+                        for a, b in ([x for x in YRUNS if x[0] in need] if YRUNS else [(s, s) for s in need]):
+                            xfer([("Y", s, c) for s in range(a, b + 1)], ("yy", col(a, c), col(b, c) + W), p, d)
                 else:
                     via = [q for q in solvers if d not in solvers and q != p and samechip(q, d) and j in doms_at[q]
                            and max(need) < min(rows_at[q])]
                     for a, b in runs(need):
                         xfer([("Y", s, c) for s in range(a, b + 1) for c in chunks(j)],
                              ("yy", col(a, j * CD), col(b, j * CD) + DW), (via or [p])[0], d)
+            if PAIR:
+                back = {}
+                for s in rows:
+                    if s and (CORES[s], ("Y", s, j * CD)) not in tok and s != N - 1:
+                        back.setdefault(chipof(CORES[s]), []).append(s)
+                for ss in back.values():
+                    fan([([("Y", s, j)], ("yy", col(s, j), col(s, j) + W), CORES[s]) for s in ss], p)
             for s in rows:
                 o = CORES[s]
                 if s == 0 or (o, ("Y", s, j * CD)) in tok:
@@ -277,8 +313,8 @@ def _build():
     def tail(op):
         k = op["kind"]
         if k == "send":
-            return NOM[1] + op["bytes"] / (NOM[2] if op["on"] else NOM[3])
-        return 2.0 + op["bytes"] / 3.0e5 if k in ("load", "store") else 0.1
+            return NOM[1] + max([op["bytes"] / (NOM[2] if op["on"] else NOM[2] / 2)] + [b / NOM[3] for b in op["lk"].values()])
+        return NOM[5] + op["bytes"] / 3.0e5 if k in ("load", "store") else 0.1
 
     indeg = [len(p) for p in par]
     topo_order = [i for i in range(n) if indeg[i] == 0]
@@ -302,9 +338,10 @@ def _build():
         if op["kind"] == "send":
             if qk not in qfree:
                 st += NOM[4]
-            port = op["core"] if op["on"] else chipof(op["dst"]) + (topo.die(op["core"]),)
-            beg = max(st + busy(op), engfree.get(op["core"], 0.0), engfree.get(port, 0.0))
-            engfree[op["core"]] = engfree[port] = beg + tail(op) - NOM[1]
+            beg = max([st + busy(op), engfree.get(op["core"], 0.0)] + [engfree.get(l, 0.0) for l in op["lk"]])
+            engfree[op["core"]] = beg + op["bytes"] / (NOM[2] if op["on"] else NOM[2] / 2)
+            for l, b in op["lk"].items():
+                engfree[l] = beg + b / NOM[3]
             done = beg + tail(op)
         else:
             done = st + busy(op) + tail(op)
@@ -335,7 +372,7 @@ def _build():
     tls = {c: {k: i for i, k in enumerate(sorted(v))} for c, v in tlp.items()}
     bbs = {c: {k: i for i, k in enumerate(sorted(v))} for c, v in bbp.items()}
     return {"span": span[0], "prog": prog, "tls": tls, "bbs": bbs, "nsem": max(semn.values()), "W": W,
-            "tln": max(len(v) for v in tls.values()), "bbn": max(len(v) for v in bbs.values()),
+            "tln": max(len(v) for v in tls.values()), "bbn": max(len(v) for v in bbs.values()), "ops": ops, "par": par,
             "banks": 1 + max(op["bank"] for op in ops if op["kind"] == "mm")}
 
 

@@ -8,12 +8,11 @@ TS = 128
 NCORES = 256
 CORES = [33, 38, 57, 62, 81, 86, 161, 166, 185, 190, 209, 214]
 
-GROUPS = [[0, 1, 2, 3, 4, 5, 6], [7, 8, 9, 10, 11]]
-HOME = [1, -1]
-P = 4
-PG = [4, 4]
-C = 4
-EXTRA = {}
+GROUPS = [[0, 1], [2, 3, 4, 5, 6, 7, 8, 9, 10, 11]]
+HOME = [1, [-1, 3]]
+P = 8
+PG = [4, 8]
+C = 8
 RELAY = "helper"
 TFWD = True
 FUSE = True
@@ -21,9 +20,10 @@ CAP_ON, CAP_OFF = 16, 8
 RET_FINE = True
 SEGS = [[1, 2], [3, 4], [5, 6], [7, 8], [9, 11]]
 DIRECT = []
-YRUNS = None
+PRUNS = [[2, 2], [3, 3], [4, 5], [6, 8], [9, 11]]
 PAIR = True
 DIEFWD = True
+XDIE = [(4, 9)]
 RELAY2 = False
 NOM = (0.4, 1.2, 4.0e5, 2.0e5, 1.0, 1.5)
 
@@ -153,38 +153,41 @@ def _build():
 
     rows_at, doms_at, sol, gidx = {}, {}, [], {}
     for gi, rows in enumerate(GROUPS):
-        lead = CORES[abs(HOME[gi])]
-        if HOME[gi] < 0:
-            lead = [c for c in range(NCORES) if topo.mates(c, lead)][0]
-        free = [c for c in range(NCORES) if samechip(c, lead) and c not in CORES
-                and all(topo.may_write(c, d) for d in CORES)]
-        od = [c for c in free if topo.die(c) != topo.die(lead)]
-        sd = [c for c in free if topo.die(c) == topo.die(lead)]
-        seq = [lead] + [x for pair in zip(od, sd + od) for x in pair]
-        if HOME[gi] < 0:
+        if gi == 0:
+            lead = CORES[HOME[gi]]
+            free = [c for c in range(NCORES) if samechip(c, lead) and c not in CORES
+                    and all(topo.may_write(c, d) for d in CORES)]
+            od = [c for c in free if topo.die(c) != topo.die(lead)]
+            sd = [c for c in free if topo.die(c) == topo.die(lead)]
+            seq = [lead] + [x for pair in zip(od, sd + od) for x in pair]
+        else:
             seq = []
             for j in range(P):
-                seq.append([c for c in free if c not in seq and topo.die(c) == topo.die(sol[0][j])][0])
+                h = HOME[gi][j * len(HOME[gi]) // P]
+                lead = CORES[abs(h)]
+                if h < 0:
+                    lead = [c for c in range(NCORES) if topo.mates(c, lead)][0]
+                seq.append([c for c in range(NCORES) if samechip(c, lead) and all(topo.may_write(c, d) for d in CORES)
+                            and c not in seq and topo.die(c) == topo.die(sol[0][j])][0])
         sol.append([seq[j * PG[gi] // P] for j in range(P)])
         for j, x in enumerate(sol[gi]):
             rows_at[x] = list(rows)
             doms_at.setdefault(x, []).append(j)
         for r in rows:
             gidx[r] = gi
-    solvers = list(rows_at)
-    for rank, rows in EXTRA.items():
-        rows_at[CORES[rank]] = list(rows)
-        doms_at[CORES[rank]] = list(range(P))
 
     def chunks(j):
         return range(j * CD, (j + 1) * CD)
 
+    def nm(r):
+        if any(samechip(CORES[r], d) for d in sol[1]):
+            return "S"
+        return "Y" if r == GROUPS[1][0] else "C"
+
     for r in range(N):
         o = CORES[r]
         if r == 0:
-            for j in range(P):
-                load(o, ("sync", "scalar")[j % 2], [("Y", 0, c) for c in chunks(j)], ("yy", col(0, j * CD), col(0, j * CD) + DW),
-                     ("b", j * DW, (j + 1) * DW))
+            load(o, "sync", [("Y", 0, c) for c in range(C)], ("bb", 0, 0, TK), ("b", 0, TK))
         else:
             load(o, "sync", [("B", r, j) for j in range(P)], ("bb", r, 0, TK), ("b", 0, TK))
         if r < N - 1:
@@ -193,30 +196,45 @@ def _build():
                 if a <= b:
                     load(o, q, [("T", r, x) for x in range(a, b + 1)], ("tl", r, a, b), ("l", a * TS, (b + 1) * TS))
 
+    fl = {}
     for s in range(N - 1):
         src = CORES[s]
         first, later = {}, []
 
-        def route(d, need):
+        def route(d, need, far=()):
             if topo.may_write(src, d):
                 first.setdefault((d, need[0]), set()).update(need)
             else:
-                rl = relay_of(src, d, True)
+                own = [c for c in range(NCORES) if c != src and samechip(c, src) and topo.may_write(c, d)
+                       and c not in CORES and topo.die(c) == topo.die(d)]
+                rl = ([c for c in far if topo.die(c) == topo.die(d)] + own)[0]
                 first.setdefault((rl, need[0]), set()).update(need)
                 later.append((rl, d, need))
 
-        sets = [sorted(set(x)) for x in sol] + [[CORES[k]] for k in EXTRA]
+        sets = []
+        for x in sol:
+            bc = {}
+            for d in sorted(set(x)):
+                bc.setdefault(chipof(d), []).append(d)
+            sets.extend(bc.values())
         for dset, seg in [(x, y) for x in sets for y in SEGS]:
-            need = [r for r in rows_at[dset[0]] if r > s and seg[0] <= r <= seg[1]]
+            need = [r for r in range(s + 1, N) if s in rows_at[dset[0]] and seg[0] <= r <= seg[1]]
             dset = [d for d in dset if d != src]
             if not need or not dset:
                 continue
             if TFWD and len(dset) > 1 and not samechip(src, dset[0]) and (s, seg[0]) not in DIRECT:
-                ld = dset[s % len(dset)]
+                ld, far, xd = dset[s % len(dset)], [], topo.die(src)
+                if not topo.may_write(src, dset[0]):
+                    far = [c for c in range(NCORES) if topo.mates(c, dset[0]) and topo.may_write(src, c)
+                           and topo.may_write(c, dset[0]) and not any(samechip(c, x) for x in list(rows_at) + CORES)]
+                    if not far and (s, seg[0]) in XDIE:
+                        xd = [topo.die(d) for d in dset if topo.die(d) != xd][0]
                 if DIEFWD:
-                    cd = [d for d in dset if topo.die(d) == topo.die(src)]
-                    ld = cd[(s // 2 + seg[0]) % len(cd)]
-                route(ld, need)
+                    cd = [d for d in dset if topo.die(d) == xd]
+                    cd = [d for d in cd if d not in CORES] or cd
+                    ld = min(cd, key=lambda d: (fl.get(d, 0), d))
+                    fl[ld] = fl.get(ld, 0) + len(need)
+                route(ld, need, far)
                 later.extend((ld, d, need) for d in dset if d != ld)
             else:
                 for d in dset:
@@ -228,50 +246,48 @@ def _build():
         for k, its in calls.items():
             sendm(its, k[0])
 
-    for k in range(CD):
-        fan([([("Y", 0, j * CD + k)], ("yy", col(0, j * CD + k), col(0, j * CD + k) + W), d)
-             for d, rows in rows_at.items() if 0 in rows and d != CORES[0] for j in doms_at[d]], CORES[0])
-    for r in range(1, N):
-        fan([([("B", r, j)], ("bb", r, j * DW, (j + 1) * DW), d)
-             for d, rows in rows_at.items() if r in rows and d != CORES[r] for j in doms_at[d]], CORES[r])
+    for r in range(N):
+        fan([([("B" if r else "Y", r, j) for j in doms_at[d]], ("bb", r, doms_at[d][0] * DW, (doms_at[d][-1] + 1) * DW), d)
+             for d, rows in rows_at.items() if (r in rows if r in GROUPS[0] or nm(r) == "S" else 0 in rows) and d != CORES[r]],
+            CORES[r])
 
     for x, rows in rows_at.items():
-        comp = [r for r in rows if r > 0]
+        first = rows[0] == 0
+        comp = [r for r in range(rows[0] + 1, N)]
         cs = [c for j in doms_at[x] for c in chunks(j)]
         nb = 8 // len(cs)
+        if not first:
+            for r in [r for r in rows if nm(r) == "S"]:
+                for c in cs:
+                    psem = newsem([x])
+                    op = addop(core=x, q="vector", kind="pre", r=r, c=c, sem=psem,
+                               deps=[(x, ("S", r, c)), (x, ("B", r, c // CD))])
+                    tok[(x, ("Y" if r == rows[0] else "C", r, c))] = (psem, 1, [op["id"]])
         for i, r in enumerate(comp):
             for ci, c in enumerate(cs):
                 sem, ids, bank = newsem([x]), [], (i % nb) * len(cs) + ci
-                for s in range(r):
+                for s in [s for s in rows if s < r]:
                     deps = [(x, ("T", s, r)), (x, ("Y", s, c))]
                     if i >= nb:
-                        deps.append((x, ("Y", comp[i - nb], c)))
+                        deps.append((x, ("Y" if comp[i - nb] in rows else nm(comp[i - nb]), comp[i - nb], c)))
                     ids.append(addop(core=x, q="tensor", kind="mm", r=r, s=s, c=c, bank=bank, sem=sem, deps=deps)["id"])
-                tok[(x, ("A", r, c))] = (sem, r, ids)
+                tok[(x, ("A", r, c))] = (sem, len(ids), ids)
                 ysem = newsem([x])
-                op = addop(core=x, q="vector", kind="sub", r=r, c=c, bank=bank, sem=ysem,
-                           deps=[(x, ("A", r, c)), (x, ("B", r, c // CD))])
-                tok[(x, ("Y", r, c))] = (ysem, 1, [op["id"]])
+                if r in rows or nm(r) != "S":
+                    op = addop(core=x, q="vector", kind="sub", r=r, c=c, bank=bank, sem=ysem, cin=not first,
+                               deps=[(x, ("A", r, c)), (x, ("B", r, c // CD) if first else ("C", r, c))])
+                    tok[(x, ("Y" if r in rows else nm(r), r, c))] = (ysem, 1, [op["id"]])
+                else:
+                    op = addop(core=x, q="vector", kind="cp", r=r, c=c, bank=bank, sem=ysem, deps=[(x, ("A", r, c))])
+                    tok[(x, ("S", r, c))] = (ysem, 1, [op["id"]])
 
     for gi, rows in enumerate(GROUPS):
         for j in range(P):
             p = sol[gi][j]
-            for d, drows in rows_at.items():
-                if d == p or j not in doms_at[d]:
-                    continue
-                need = [s for s in rows if s not in drows and s < max(drows) and not (s == 0 and d == CORES[0])]
-                if not need:
-                    continue
-                if min(drows) - 1 in rows:
-                    for c in chunks(j):
-                        for a, b in ([x for x in YRUNS if x[0] in need] if YRUNS else [(s, s) for s in need]):
-                            xfer([("Y", s, c) for s in range(a, b + 1)], ("yy", col(a, c), col(b, c) + W), p, d)
-                else:
-                    via = [q for q in solvers if d not in solvers and q != p and samechip(q, d) and j in doms_at[q]
-                           and max(need) < min(rows_at[q])]
-                    for a, b in runs(need):
-                        xfer([("Y", s, c) for s in range(a, b + 1) for c in chunks(j)],
-                             ("yy", col(a, j * CD), col(b, j * CD) + DW), (via or [p])[0], d)
+            if gi == 0 and j == doms_at[p][0]:
+                for a, b in PRUNS:
+                    fan([([(nm(r), r, k) for r in range(a, b + 1)], ("yy", col(a, k), col(b, k) + W), sol[1][k])
+                         for k in doms_at[p]], p)
             if PAIR:
                 back = {}
                 for s in rows:
@@ -291,6 +307,9 @@ def _build():
 
     for r in range(N):
         o, c, k = CORES[r], 0, 0
+        if r == 0:
+            addop(core=o, q="scalar", kind="store", a=0, b=TK, ya=None, deps=[(o, ("Y", 0, 0))], bytes=TK * 256)
+            continue
         while c < C:
             e = c
             while e + 1 < C and (e + 1) // CD == c // CD and tok[(o, ("Y", r, e + 1))][0] == tok[(o, ("Y", r, c))][0]:
@@ -308,7 +327,8 @@ def _build():
 
     def busy(op):
         k = op["kind"]
-        return NOM[0] if k == "send" else W / 1400.0 + 0.06 if k == "mm" else W / 960.0 + 0.06 if k == "sub" else 0.05
+        return (NOM[0] if k == "send" else W / 1400.0 + 0.06 if k == "mm"
+                else W / 960.0 + 0.06 if k in ("sub", "cp", "pre") else 0.05)
 
     def tail(op):
         k = op["kind"]
@@ -367,7 +387,7 @@ def _build():
             op["stop"] = True
     for op in ops:
         op["waits"] = sorted({tok[d][:2] for d in op["deps"]})
-        if op["kind"] in ("mm", "sub"):
+        if op["kind"] in ("mm", "sub", "cp", "pre"):
             op["yc"] = col(op["s"] if op["kind"] == "mm" else op["r"], op["c"])
     tls = {c: {k: i for i, k in enumerate(sorted(v))} for c, v in tlp.items()}
     bbs = {c: {k: i for i, k in enumerate(sorted(v))} for c, v in bbp.items()}
@@ -416,7 +436,9 @@ def rank_program(g, core, T, topo):
                 src = T.b if op["src"][0] == "b" else T.l
                 q.dma_start(ap(core, op["spec"]), src[:, op["src"][1]:op["src"][2]]).then_inc(T.sem["s%d" % op["sem"]], 16)
             elif kind == "store":
-                q.dma_start(T.y[:, op["a"]:op["b"]], T.yy[:, op["ya"]:op["ya"] + op["b"] - op["a"]]).then_inc(T.sem["st" + qn], 16)
+                k = _P["bbs"][core][0] * TK if op["ya"] is None else 0
+                q.dma_start(T.y[:, op["a"]:op["b"]], T.bb[:, k:k + TK] if op["ya"] is None else
+                            T.yy[:, op["ya"]:op["ya"] + op["b"] - op["a"]]).then_inc(T.sem["st" + qn], 16)
                 stored += 16
             elif kind == "send":
                 m = -1
@@ -441,13 +463,22 @@ def rank_program(g, core, T, topo):
                     q.remote_dma_fused(trs, local_sem=T.sem.sent)
             elif kind == "mm":
                 k = _P["tls"][core][(op["s"], op["r"])]
-                q.matmul(T["ps%d" % op["bank"]][:, 0:W], T.tl[:, k * TS:(k + 1) * TS], T.yy[:, op["yc"]:op["yc"] + W],
+                k0 = _P["bbs"][core][0] * TK + op["c"] * W if op["s"] == 0 else 0
+                q.matmul(T["ps%d" % op["bank"]][:, 0:W], T.tl[:, k * TS:(k + 1) * TS],
+                         T.bb[:, k0:k0 + W] if op["s"] == 0 else T.yy[:, op["yc"]:op["yc"] + W],
                          start=op["start"], stop=op["stop"]).then_inc(T.sem["s%d" % op["sem"]], 1)
+            elif kind == "cp":
+                q.tensor_copy(out=T.yy[:, op["yc"]:op["yc"] + W], in_=T["ps%d" % op["bank"]][:, 0:W]
+                              ).then_inc(T.sem["s%d" % op["sem"]], 1)
             else:
-                k = _P["bbs"][core][op["r"]] * TK + op["c"] * W
-                q.tensor_tensor(out=T.yy[:, op["yc"]:op["yc"] + W], in0=T.bb[:, k:k + W],
-                                in1=T["ps%d" % op["bank"]][:, 0:W], op=AluOpType.subtract
-                                ).then_inc(T.sem["s%d" % op["sem"]], 1)
+                here = T.yy[:, op["yc"]:op["yc"] + W]
+                if kind == "sub" and op["cin"]:
+                    in0 = here
+                else:
+                    k = _P["bbs"][core][op["r"]] * TK + op["c"] * W
+                    in0 = T.bb[:, k:k + W]
+                q.tensor_tensor(out=here, in0=in0, in1=here if kind == "pre" else T["ps%d" % op["bank"]][:, 0:W],
+                                op=AluOpType.subtract).then_inc(T.sem["s%d" % op["sem"]], 1)
         if sent:
             q.wait_ge(T.sem.sent, sent)
         if stored:

import comms_topo
from concourse.bass import DstId, RemoteDMATransfer
from concourse.mybir import AluOpType

N = 12
TK = 512
TS = 128
NCORES = 256
CORES = [33, 38, 57, 62, 81, 86, 161, 166, 185, 190, 209, 214]

GROUPS = [[0, 1], [2, 3, 4, 5, 6, 7, 8, 9, 10, 11]]
HOME = [1, [-1, 3]]
P = 8
PG = [4, 8]
C = 8
RELAY = "helper"
TFWD = True
FUSE = True
CAP_ON, CAP_OFF = 16, 8
RET_FINE = True
SEGS = [[1, 2], [3, 4], [5, 6], [7, 8], [9, 11]]
DIRECT = []
PRUNS = [[2, 2], [3, 3], [4, 5], [6, 8], [9, 11]]
PAIR = True
DIEFWD = True
XDIE = [(4, 9)]
RELAY2 = False
NOM = (0.4, 1.2, 4.0e5, 2.0e5, 1.0, 1.5)


def _bits(m):
    return [i for i in range(32) if (m >> i) & 1]


def _build():
    topo = comms_topo
    W, CD, DW = TK // C, C // P, TK // P
    ops, tok, semn, tlp, bbp = [], {}, {}, {}, {}

    def col(r, c):
        return ((c // CD) * N + r) * DW + (c % CD) * W

    def newsem(cores):
        i = max(semn.get(c, 0) for c in cores)
        for c in cores:
            semn[c] = i + 1
        return i

    def addop(**kw):
        kw["id"] = len(ops)
        kw.setdefault("deps", [])
        ops.append(kw)
        return kw

    def chipof(a):
        return (topo.host(a), topo.chip(a))

    def samechip(a, b):
        return chipof(a) == chipof(b)

    def relay_of(src, dst, alt=False):
        cand = [c for c in range(NCORES) if c != src and samechip(c, src) and topo.may_write(c, dst)]
        if RELAY == "rank":
            pref = [c for c in cand if c in CORES]
        else:
            pref = [c for c in cand if c not in CORES and topo.die(c) == topo.die(src)]
        return (pref or cand)[-1 if alt and RELAY2 else 0]

    def links(src, dst):
        if samechip(src, dst):
            return []
        d = topo.die(src)
        if topo.same_plane(src, dst):
            return [("out", chipof(src), d), ("in", chipof(dst), d)]
        mt = chipof([c for c in range(NCORES) if topo.mates(c, src)][0])
        if mt == chipof(dst):
            return [("mate", chipof(src), d)]
        return [("mate", chipof(src), d), ("out", mt, d), ("in", chipof(dst), d)]

    def width(spec):
        return (spec[3] - spec[2] + 1) * TS if spec[0] == "tl" else spec[-1] - spec[-2]

    def present(core, spec):
        if spec[0] == "bb":
            bbp.setdefault(core, set()).add(spec[1])
        elif spec[0] == "tl":
            for r in range(spec[2], spec[3] + 1):
                tlp.setdefault(core, set()).add((spec[1], r))

    def sendm(items, src):
        if not FUSE and len(items) > 1:
            for it in items:
                sendm([it], src)
            return
        byspec, m = {}, -1
        for keys, spec, dst in items:
            byspec.setdefault(spec, (keys, []))[1].append(dst)
            m &= topo.mask(src, dst)
        on = all(samechip(src, it[2]) for it in items)
        cap, ne = min(len(_bits(m)), CAP_ON if on else CAP_OFF), 1
        while ne * 2 * len(byspec) <= cap:
            ne *= 2
        op = addop(core=src, q="g", kind="send", deps=sorted({(src, k) for it in items for k in it[0]}), trs=[], on=on,
                   dst=items[0][2], bytes=sum(width(it[1]) * 256 for it in items), lk={})
        for it in items:
            for l in links(src, it[2]):
                op["lk"][l] = op["lk"].get(l, 0) + width(it[1]) * 256
        for i, (spec, (keys, dsts)) in enumerate(byspec.items()):
            sem = newsem(dsts)
            op["trs"].append({"spec": spec, "dsts": dsts, "sem": sem, "ne": ne, "off": i * ne})
            for d in dsts:
                for k in keys:
                    assert (d, k) not in tok, (d, k)
                    tok[(d, k)] = (sem, ne, [op["id"]])
                present(d, spec)

    def bychip(items, src):
        grp = {}
        for it in items:
            grp.setdefault(chipof(it[2]), []).append(it)
        for its in grp.values():
            sendm(its, src)

    def fan(items, src):
        items = [it for it in items if not all((it[2], k) in tok for k in it[0])]
        bychip([it for it in items if topo.may_write(src, it[2])], src)
        rel = {}
        for it in items:
            if not topo.may_write(src, it[2]):
                rel.setdefault(relay_of(src, it[2]), []).append(it)
        for rl, its in rel.items():
            fan(list({it[1]: (it[0], it[1], rl) for it in its}.values()), src)
            bychip(its, rl)

    def xfer(keys, spec, src, dst):
        fan([(keys, spec, dst)], src)

    def load(core, q, keys, spec, src):
        sem = newsem([core])
        op = addop(core=core, q=q, kind="load", spec=spec, src=src, sem=sem, bytes=width(spec) * 256)
        for k in keys:
            tok[(core, k)] = (sem, 16, [op["id"]])
        present(core, spec)

    def runs(rows):
        out = []
        for r in sorted(rows):
            if out and out[-1][1] == r - 1:
                out[-1][1] = r
            else:
                out.append([r, r])
        return out

    rows_at, doms_at, sol, gidx = {}, {}, [], {}
    for gi, rows in enumerate(GROUPS):
        if gi == 0:
            lead = CORES[HOME[gi]]
            free = [c for c in range(NCORES) if samechip(c, lead) and c not in CORES
                    and all(topo.may_write(c, d) for d in CORES)]
            od = [c for c in free if topo.die(c) != topo.die(lead)]
            sd = [c for c in free if topo.die(c) == topo.die(lead)]
            seq = [lead] + [x for pair in zip(od, sd + od) for x in pair]
        else:
            seq = []
            for j in range(P):
                h = HOME[gi][j * len(HOME[gi]) // P]
                lead = CORES[abs(h)]
                if h < 0:
                    lead = [c for c in range(NCORES) if topo.mates(c, lead)][0]
                seq.append([c for c in range(NCORES) if samechip(c, lead) and all(topo.may_write(c, d) for d in CORES)
                            and c not in seq and topo.die(c) == topo.die(sol[0][j])][0])
        sol.append([seq[j * PG[gi] // P] for j in range(P)])
        for j, x in enumerate(sol[gi]):
            rows_at[x] = list(rows)
            doms_at.setdefault(x, []).append(j)
        for r in rows:
            gidx[r] = gi

    def chunks(j):
        return range(j * CD, (j + 1) * CD)

    def nm(r):
        if any(samechip(CORES[r], d) for d in sol[1]):
            return "S"
        return "Y" if r == GROUPS[1][0] else "C"

    for r in range(N):
        o = CORES[r]
        if r == 0:
            load(o, "sync", [("Y", 0, c) for c in range(C)], ("bb", 0, 0, TK), ("b", 0, TK))
        else:
            load(o, "sync", [("B", r, j) for j in range(P)], ("bb", r, 0, TK), ("b", 0, TK))
        if r < N - 1:
            for i, (a, b) in enumerate([(max(x[0], r + 1), x[1]) for x in SEGS if x[1] > r]):
                q = ("scalar", "sync")[i % 2]
                if a <= b:
                    load(o, q, [("T", r, x) for x in range(a, b + 1)], ("tl", r, a, b), ("l", a * TS, (b + 1) * TS))

    fl = {}
    for s in range(N - 1):
        src = CORES[s]
        first, later = {}, []

        def route(d, need, far=()):
            if topo.may_write(src, d):
                first.setdefault((d, need[0]), set()).update(need)
            else:
                own = [c for c in range(NCORES) if c != src and samechip(c, src) and topo.may_write(c, d)
                       and c not in CORES and topo.die(c) == topo.die(d)]
                rl = ([c for c in far if topo.die(c) == topo.die(d)] + own)[0]
                first.setdefault((rl, need[0]), set()).update(need)
                later.append((rl, d, need))

        sets = []
        for x in sol:
            bc = {}
            for d in sorted(set(x)):
                bc.setdefault(chipof(d), []).append(d)
            sets.extend(bc.values())
        for dset, seg in [(x, y) for x in sets for y in SEGS]:
            need = [r for r in range(s + 1, N) if s in rows_at[dset[0]] and seg[0] <= r <= seg[1]]
            dset = [d for d in dset if d != src]
            if not need or not dset:
                continue
            if TFWD and len(dset) > 1 and not samechip(src, dset[0]) and (s, seg[0]) not in DIRECT:
                ld, far, xd = dset[s % len(dset)], [], topo.die(src)
                if not topo.may_write(src, dset[0]):
                    far = [c for c in range(NCORES) if topo.mates(c, dset[0]) and topo.may_write(src, c)
                           and topo.may_write(c, dset[0]) and not any(samechip(c, x) for x in list(rows_at) + CORES)]
                    if not far and (s, seg[0]) in XDIE:
                        xd = [topo.die(d) for d in dset if topo.die(d) != xd][0]
                if DIEFWD:
                    cd = [d for d in dset if topo.die(d) == xd]
                    cd = [d for d in cd if d not in CORES] or cd
                    ld = min(cd, key=lambda d: (fl.get(d, 0), d))
                    fl[ld] = fl.get(ld, 0) + len(need)
                route(ld, need, far)
                later.extend((ld, d, need) for d in dset if d != ld)
            else:
                for d in dset:
                    route(d, need)
        calls = {}
        for f, d, rows in [(src, d[0], rows) for d, rows in first.items()] + later:
            for a, b in runs(rows):
                calls.setdefault((f, a, b, chipof(d)), []).append(([("T", s, x) for x in range(a, b + 1)], ("tl", s, a, b), d))
        for k, its in calls.items():
            sendm(its, k[0])

    for r in range(N):
        fan([([("B" if r else "Y", r, j) for j in doms_at[d]], ("bb", r, doms_at[d][0] * DW, (doms_at[d][-1] + 1) * DW), d)
             for d, rows in rows_at.items() if (r in rows if r in GROUPS[0] or nm(r) == "S" else 0 in rows) and d != CORES[r]],
            CORES[r])

    for x, rows in rows_at.items():
        first = rows[0] == 0
        comp = [r for r in range(rows[0] + 1, N)]
        cs = [c for j in doms_at[x] for c in chunks(j)]
        nb = 8 // len(cs)
        if not first:
            for r in [r for r in rows if nm(r) == "S"]:
                for c in cs:
                    psem = newsem([x])
                    op = addop(core=x, q="vector", kind="pre", r=r, c=c, sem=psem,
                               deps=[(x, ("S", r, c)), (x, ("B", r, c // CD))])
                    tok[(x, ("Y" if r == rows[0] else "C", r, c))] = (psem, 1, [op["id"]])
        for i, r in enumerate(comp):
            for ci, c in enumerate(cs):
                sem, ids, bank = newsem([x]), [], (i % nb) * len(cs) + ci
                for s in [s for s in rows if s < r]:
                    deps = [(x, ("T", s, r)), (x, ("Y", s, c))]
                    if i >= nb:
                        deps.append((x, ("Y" if comp[i - nb] in rows else nm(comp[i - nb]), comp[i - nb], c)))
                    ids.append(addop(core=x, q="tensor", kind="mm", r=r, s=s, c=c, bank=bank, sem=sem, deps=deps)["id"])
                tok[(x, ("A", r, c))] = (sem, len(ids), ids)
                ysem = newsem([x])
                if r in rows or nm(r) != "S":
                    op = addop(core=x, q="vector", kind="sub", r=r, c=c, bank=bank, sem=ysem, cin=not first,
                               deps=[(x, ("A", r, c)), (x, ("B", r, c // CD) if first else ("C", r, c))])
                    tok[(x, ("Y" if r in rows else nm(r), r, c))] = (ysem, 1, [op["id"]])
                else:
                    op = addop(core=x, q="vector", kind="cp", r=r, c=c, bank=bank, sem=ysem, deps=[(x, ("A", r, c))])
                    tok[(x, ("S", r, c))] = (ysem, 1, [op["id"]])

    for gi, rows in enumerate(GROUPS):
        for j in range(P):
            p = sol[gi][j]
            if gi == 0 and j == doms_at[p][0]:
                for a, b in PRUNS:
                    fan([([(nm(r), r, k) for r in range(a, b + 1)], ("yy", col(a, k), col(b, k) + W), sol[1][k])
                         for k in doms_at[p]], p)
            if PAIR:
                back = {}
                for s in rows:
                    if s and (CORES[s], ("Y", s, j * CD)) not in tok and s != N - 1:
                        back.setdefault(chipof(CORES[s]), []).append(s)
                for ss in back.values():
                    fan([([("Y", s, j)], ("yy", col(s, j), col(s, j) + W), CORES[s]) for s in ss], p)
            for s in rows:
                o = CORES[s]
                if s == 0 or (o, ("Y", s, j * CD)) in tok:
                    continue
                if RET_FINE:
                    for c in chunks(j):
                        xfer([("Y", s, c)], ("yy", col(s, c), col(s, c) + W), p, o)
                else:
                    xfer([("Y", s, c) for c in chunks(j)], ("yy", col(s, j * CD), col(s, j * CD) + DW), p, o)

    for r in range(N):
        o, c, k = CORES[r], 0, 0
        if r == 0:
            addop(core=o, q="scalar", kind="store", a=0, b=TK, ya=None, deps=[(o, ("Y", 0, 0))], bytes=TK * 256)
            continue
        while c < C:
            e = c
            while e + 1 < C and (e + 1) // CD == c // CD and tok[(o, ("Y", r, e + 1))][0] == tok[(o, ("Y", r, c))][0]:
                e += 1
            addop(core=o, q=("sync", "scalar")[k % 2], kind="store", a=c * W, b=(e + 1) * W, ya=col(r, c),
                  deps=[(o, ("Y", r, c))], bytes=(e + 1 - c) * W * 256)
            c, k = e + 1, k + 1

    n = len(ops)
    par = [sorted({i for d in op["deps"] for i in tok[d][2]}) for op in ops]
    chi = [[] for _ in ops]
    for i, ps in enumerate(par):
        for p in ps:
            chi[p].append(i)

    def busy(op):
        k = op["kind"]
        return (NOM[0] if k == "send" else W / 1400.0 + 0.06 if k == "mm"
                else W / 960.0 + 0.06 if k in ("sub", "cp", "pre") else 0.05)

    def tail(op):
        k = op["kind"]
        if k == "send":
            return NOM[1] + max([op["bytes"] / (NOM[2] if op["on"] else NOM[2] / 2)] + [b / NOM[3] for b in op["lk"].values()])
        return NOM[5] + op["bytes"] / 3.0e5 if k in ("load", "store") else 0.1

    indeg = [len(p) for p in par]
    topo_order = [i for i in range(n) if indeg[i] == 0]
    for i in topo_order:
        for ch in chi[i]:
            indeg[ch] -= 1
            if indeg[ch] == 0:
                topo_order.append(ch)
    assert len(topo_order) == n
    bl = [0.0] * n
    for i in reversed(topo_order):
        bl[i] = busy(ops[i]) + tail(ops[i]) + max([bl[ch] for ch in chi[i]] or [0.0])
    indeg = [len(p) for p in par]
    ready = {i: 0.0 for i in range(n) if indeg[i] == 0}
    rdy, qfree, engfree, prog, span = [0.0] * n, {}, {}, {}, [0.0]
    while ready:
        best = min(ready, key=lambda i: (max(ready[i], qfree.get((ops[i]["core"], ops[i]["q"]), 0.0)), -bl[i], i))
        op = ops[best]
        qk = (op["core"], op["q"])
        st = max(ready.pop(best), qfree.get(qk, 0.0))
        if op["kind"] == "send":
            if qk not in qfree:
                st += NOM[4]
            beg = max([st + busy(op), engfree.get(op["core"], 0.0)] + [engfree.get(l, 0.0) for l in op["lk"]])
            engfree[op["core"]] = beg + op["bytes"] / (NOM[2] if op["on"] else NOM[2] / 2)
            for l, b in op["lk"].items():
                engfree[l] = beg + b / NOM[3]
            done = beg + tail(op)
        else:
            done = st + busy(op) + tail(op)
        qfree[qk] = st + busy(op)
        span[0] = max(span[0], done)
        op["t0"], op["t1"] = st, done
        prog.setdefault(op["core"], {}).setdefault(op["q"], []).append(op)
        for ch in chi[best]:
            rdy[ch] = max(rdy[ch], done)
            indeg[ch] -= 1
            if indeg[ch] == 0:
                ready[ch] = rdy[ch]

    for core, qs in prog.items():
        seen, last = set(), {}
        for op in qs.get("tensor", []):
            k = (op["r"], op["c"])
            op["start"] = k not in seen
            op["stop"] = False
            seen.add(k)
            last[k] = op
        for op in last.values():
            op["stop"] = True
    for op in ops:
        op["waits"] = sorted({tok[d][:2] for d in op["deps"]})
        if op["kind"] in ("mm", "sub", "cp", "pre"):
            op["yc"] = col(op["s"] if op["kind"] == "mm" else op["r"], op["c"])
    tls = {c: {k: i for i, k in enumerate(sorted(v))} for c, v in tlp.items()}
    bbs = {c: {k: i for i, k in enumerate(sorted(v))} for c, v in bbp.items()}
    return {"span": span[0], "prog": prog, "tls": tls, "bbs": bbs, "nsem": max(semn.values()), "W": W,
            "tln": max(len(v) for v in tls.values()), "bbn": max(len(v) for v in bbs.values()), "ops": ops, "par": par,
            "banks": 1 + max(op["bank"] for op in ops if op["kind"] == "mm")}


_P = _build()

SCRATCH = {
    "yy": ("sbuf", [128, N * TK], "bfloat16"),
    "bb": ("sbuf", [128, _P["bbn"] * TK], "bfloat16"),
    "tl": ("sbuf", [128, _P["tln"] * TS], "bfloat16"),
}
for _i in range(_P["banks"]):
    SCRATCH["ps%d" % _i] = ("psum", [128, 512], "float32")
SEMAPHORES = ["sent", "stsync", "stscalar"] + ["s%d" % _i for _i in range(_P["nsem"])]


def rank_program(g, core, T, topo):
    prog = _P["prog"].get(core)
    if not prog:
        return
    W = _P["W"]
    queues = {"g": g, "tensor": g.tensor, "vector": g.vector, "sync": g.sync, "scalar": g.scalar}

    def ap(c, spec):
        if spec[0] == "yy":
            return T.yy[:, spec[1]:spec[2]]
        if spec[0] == "bb":
            k = _P["bbs"][c][spec[1]] * TK
            return T.bb[:, k + spec[2]:k + spec[3]]
        k = _P["tls"][c][(spec[1], spec[2])]
        return T.tl[:, k * TS:(k + spec[3] - spec[2] + 1) * TS]

    for qn, lst in prog.items():
        q, waited, sent, stored = queues[qn], {}, 0, 0
        for op in lst:
            for sem, val in op["waits"]:
                if waited.get(sem, 0) < val:
                    q.wait_ge(T.sem["s%d" % sem], val)
                    waited[sem] = val
            kind = op["kind"]
            if kind == "load":
                src = T.b if op["src"][0] == "b" else T.l
                q.dma_start(ap(core, op["spec"]), src[:, op["src"][1]:op["src"][2]]).then_inc(T.sem["s%d" % op["sem"]], 16)
            elif kind == "store":
                k = _P["bbs"][core][0] * TK if op["ya"] is None else 0
                q.dma_start(T.y[:, op["a"]:op["b"]], T.bb[:, k:k + TK] if op["ya"] is None else
                            T.yy[:, op["ya"]:op["ya"] + op["b"] - op["a"]]).then_inc(T.sem["st" + qn], 16)
                stored += 16
            elif kind == "send":
                m = -1
                for tr in op["trs"]:
                    for d in tr["dsts"]:
                        m &= topo.mask(core, d)
                eng, trs = _bits(m), []
                for tr in op["trs"]:
                    mask = sum(1 << e for e in eng[tr["off"]:tr["off"] + tr["ne"]])
                    sent += tr["ne"]
                    if len(op["trs"]) == 1 and len(tr["dsts"]) == 1:
                        rid, pid = topo.addr(tr["dsts"][0], core)
                        q.remote_dma(out_ap=ap(tr["dsts"][0], tr["spec"]), in_ap=ap(core, tr["spec"]),
                                     remote_sem=T.sem["s%d" % tr["sem"]], local_sem=T.sem.sent, pid=pid, routing_id=rid,
                                     dma_engine_mask=mask)
                    else:
                        ids = [topo.addr(d, core) for d in tr["dsts"]]
                        trs.append(RemoteDMATransfer(dst_ids=[DstId(rid=a, pnc=b) for a, b in ids], dma_engine_mask=mask,
                                                     remote_sem=T.sem["s%d" % tr["sem"]], srcs=[ap(core, tr["spec"])],
                                                     dsts=[ap(d, tr["spec"]) for d in tr["dsts"]], alu_op=0))
                if trs:
                    q.remote_dma_fused(trs, local_sem=T.sem.sent)
            elif kind == "mm":
                k = _P["tls"][core][(op["s"], op["r"])]
                k0 = _P["bbs"][core][0] * TK + op["c"] * W if op["s"] == 0 else 0
                q.matmul(T["ps%d" % op["bank"]][:, 0:W], T.tl[:, k * TS:(k + 1) * TS],
                         T.bb[:, k0:k0 + W] if op["s"] == 0 else T.yy[:, op["yc"]:op["yc"] + W],
                         start=op["start"], stop=op["stop"]).then_inc(T.sem["s%d" % op["sem"]], 1)
            elif kind == "cp":
                q.tensor_copy(out=T.yy[:, op["yc"]:op["yc"] + W], in_=T["ps%d" % op["bank"]][:, 0:W]
                              ).then_inc(T.sem["s%d" % op["sem"]], 1)
            else:
                here = T.yy[:, op["yc"]:op["yc"] + W]
                if kind == "sub" and op["cin"]:
                    in0 = here
                else:
                    k = _P["bbs"][core][op["r"]] * TK + op["c"] * W
                    in0 = T.bb[:, k:k + W]
                q.tensor_tensor(out=here, in0=in0, in1=here if kind == "pre" else T["ps%d" % op["bank"]][:, 0:W],
                                op=AluOpType.subtract).then_inc(T.sem["s%d" % op["sem"]], 1)
        if sent:
            q.wait_ge(T.sem.sent, sent)
        if stored:
            q.wait_ge(T.sem["st" + qn], stored)
